import numpy as np
import ml_dtypes


def mxq(x, axis, fmt="e4m3"):
    dtype, down = {"e4m3": (ml_dtypes.float8_e4m3fn, 7), "e5m2": (ml_dtypes.float8_e5m2, 14)}[fmt]
    v = np.moveaxis(np.asarray(x, np.float32).astype(ml_dtypes.bfloat16).astype(np.float64), axis, -1)
    blocks = v.reshape(v.shape[:-1] + (-1, 32))
    amax = np.abs(blocks).max(-1, keepdims=True)
    byte = np.maximum(np.where(amax > 0, np.frexp(amax)[1] - 1 + 127, 0) - down, 1)
    scale = np.exp2(byte - 127.0)
    codes = (blocks / scale).astype(np.float32).astype(dtype).astype(np.float64)
    return np.moveaxis((codes * scale).reshape(v.shape), -1, axis)


WIDE = False


def mx_kscale(k):
    if not WIDE:
        return np.ones(k)
    levels = np.array([10, -10, 5, -5, 0])
    if k % 512:
        return np.exp2(np.random.permutation(np.resize(levels, k // 32))).repeat(32)
    a = np.empty((k // 512, 16))
    for p in range(k // 512):
        a[p, :8] = np.random.permutation(np.resize(levels, 8))
        for g in range(8):
            far = levels[np.abs(levels - a[p, g]) >= 10]
            a[p, g + 8] = far[np.random.randint(len(far))]
    return np.exp2(a.ravel()).repeat(32)


def f64(x):
    return np.asarray(x).astype(np.float64)


def striped(idx):
    return np.tile(idx.reshape(-1, 16).T, (8, 1)).astype(np.uint16)


def unstriped(offs):
    return offs[:16].T.reshape(-1).astype(np.int64)


E2M1 = np.array([0.0, 0.5, 1.0, 1.5, 2.0, 3.0, 4.0, 6.0, -0.0, -0.5, -1.0, -1.5, -2.0, -3.0, -4.0, -6.0])


def pack_weight(w, fmt):
    k, n = w.shape
    w = f64(np.asarray(w, np.float32).astype(ml_dtypes.bfloat16)).reshape(k // 32, 32, n)
    amax = np.abs(w).max(1)
    if fmt == "e4m3":
        byte = np.frexp(amax)[1] - 1 + 127 - 7
    else:
        mant, ex = np.frexp(amax / 6.0)
        byte = np.where(mant > 0.5, ex, ex - 1) + 127
    byte = np.clip(np.where(amax > 0, byte, 1), 1, 254)
    scaled = (w * np.exp2(127.0 - byte)[:, None, :]).reshape(k, n).astype(np.float32)
    by_word = np.ascontiguousarray(scaled.reshape(k // 512, 128, 4, n).transpose(0, 1, 3, 2))
    if fmt == "e4m3":
        words = by_word.astype(ml_dtypes.float8_e4m3fn).view(np.uint8)
    else:
        c = by_word.astype(ml_dtypes.float4_e2m1fn).view(np.uint8) & 0xF
        words = (c[..., 0::2] | (c[..., 1::2] << 4)).reshape(k // 512, 128, 2 * n)
    return np.ascontiguousarray(words), np.ascontiguousarray(byte.astype(np.uint8).reshape(k // 512, 16, n))


def unpack_weight(words, scales, fmt):
    g, _, n = scales.shape
    words = np.ascontiguousarray(words).reshape(g, 128, n, -1)
    if fmt == "e4m3":
        vals = words.view(ml_dtypes.float8_e4m3fn).astype(np.float64)
    else:
        nib = np.empty((g, 128, n, 4), np.uint8)
        nib[..., 0::2] = words & 0xF
        nib[..., 1::2] = words >> 4
        vals = E2M1[nib]
    vals = vals * np.repeat(np.exp2(scales.astype(np.float64) - 127.0), 8, axis=1)[..., None]
    return vals.transpose(0, 1, 3, 2).reshape(g * 512, n)


def gelu(v):
    return 0.5 * v * (1.0 + np.tanh(np.sqrt(2.0 / np.pi) * (v + 0.044715 * v**3)))


K, H, T, S, T2, P = 512, 1024, 4096, 1024, 2048, 1024

def setup_inputs():
    n = np.random.standard_normal
    s = mx_kscale(K)[:, None]
    u = mx_kscale(H)[:, None]
    d = {}
    d["tab_words"], d["tab_scales"] = pack_weight(n((K, T)) * s, "e4m3")
    d["offs"] = striped(np.random.permutation(T)[:S])
    d["w1"] = (n((K, H)) / K**0.5 / s).astype(np.float32)
    d["w4_words"], d["w4_scales"] = pack_weight(n((K, H)) / K**0.5 / s, "e2m1")
    d["light"] = (1.1 * n((H, S)) * u).astype(np.float32)
    d["page0"] = (n((H, T2)) * u).astype(np.float32)
    d["wgs"] = np.exp(0.3 * n((128, S))).astype(np.float32)
    d["offs2"] = striped(np.random.permutation(T2)[:S])
    d["sc"] = (2.0 * np.exp(0.2 * n(H)) / u[:, 0]).astype(np.float32)
    d["offs3"] = striped(np.random.permutation(T2)[:P])
    d["gain"] = (np.exp(0.3 * n(H)) * u[:, 0]).astype(np.float32)
    d["w2"] = (n((H, H)) / H**0.5 / u).astype(np.float32)
    d["offs4"] = striped(np.random.permutation(T2)[:P])
    d["base"] = (0.7 * n((H, P))).astype(np.float32)
    return d

def reference(tab_words, tab_scales, offs, w1, w4_words, w4_scales, light, page0, wgs, offs2, sc, offs3, gain, w2, offs4, base):
    v = unpack_weight(tab_words, tab_scales, "e4m3")[:, unstriped(offs)]
    grain = mxq(f64(w1), 0, "e4m3").T @ v
    flaw = unpack_weight(w4_words, w4_scales, "e2m1").T @ v
    h = np.maximum(grain, flaw) * f64(light)
    page = f64(page0).copy()
    page[:, unstriped(offs2)] = np.tile(f64(wgs), (H // 128, 1)) * h
    page = page * f64(sc)[:, None]
    x = page[:, unstriped(offs3)]
    x = f64(gain)[:, None] / (1.0 + np.exp(-x))
    y = mxq(f64(w2), 0, "e4m3").T @ mxq(x, 0, "e4m3")
    herd = page[:, unstriped(offs4)]
    return y * herd + f64(base)

@@ -1,0 +1,245 @@
+from contextlib import ExitStack
+
+import concourse.mybir as mybir
+
+K, H, T, S, T2, NP = 512, 1024, 4096, 1024, 2048, 1024
+FLOPS = 2 * (2 * K * H * S + H * H * NP)
+
+F32 = mybir.dt.float32
+BF16 = mybir.dt.bfloat16
+I32 = mybir.dt.int32
+U32 = mybir.dt.uint32
+U16 = mybir.dt.uint16
+U8 = mybir.dt.uint8
+FP8X4 = mybir.dt.float8_e4m3fn_x4
+FP4X4 = mybir.dt.float4_e2m1fn_x4
+ACT = mybir.ActivationFunctionType
+ALU = mybir.AluOpType
+
+P = 128
+PACK = 4
+KP = P * PACK
+HALF = 512
+NB = H // KP
+NS = NB * PACK
+
+
+def tile_list_hide_grading_board_kernel(tc, tab_words, tab_scales, offs, w1, w4_words, w4_scales, light, page0,
+                                                 wgs, offs2, sc, offs3, gain, w2, offs4, base, out):
+    nc = tc.nc
+    hcols = [slice(h * HALF, (h + 1) * HALF) for h in range(2)]
+    hoffs = [slice(h * HALF // 16, (h + 1) * HALF // 16) for h in range(2)]
+
+    def rows(ap, s):
+        b, t = divmod(s, PACK)
+        return ap.rearrange("(b p t) c -> b t p c", b=NB, t=PACK)[b, t]
+
+    with ExitStack() as ctx:
+        keep = ctx.enter_context(tc.tile_pool(name="keep", bufs=1))
+        ring = ctx.enter_context(tc.tile_pool(name="ring", bufs=2))
+        psum = ctx.enter_context(tc.psum_pool(name="psum", bufs=8))
+
+        l_tab = keep.tile([P, S // 16], U16, name="l_tab")
+        l_put = keep.tile([P, S // 16], U16, name="l_put")
+        l_dye = keep.tile([P, NP // 16], U16, name="l_dye")
+        l_herd = keep.tile([P, NP // 16], U16, name="l_herd")
+
+        w4s_raw = keep.tile([P, H], U8, name="w4s_raw", align_bytes=64)
+        tabs = keep.tile([P, T], U8, name="tabs", align_bytes=64)
+        nc.vector.memset(w4s_raw[:].bitcast(I32), 0)
+        nc.vector.memset(tabs[:].bitcast(I32), 0)
+        nc.sync.dma_start(l_tab[:], offs)
+        w4_raw = keep.tile([P, 2 * H], U8, name="w4_raw", align_bytes=64)
+        nc.sync.dma_start(out=w4_raw[:].bitcast(I32), in_=w4_words[0].bitcast(I32))
+        nc.sync.dma_start(l_put[:], offs2)
+        nc.sync.dma_start(l_dye[:], offs3)
+        nc.sync.dma_start(l_herd[:], offs4)
+        sc_sb = keep.tile([P, NB, PACK], F32, name="sc_sb")
+        gain_sb = keep.tile([P, NB, PACK], F32, name="gain_sb")
+        nc.sync.dma_start(out=sc_sb[:], in_=sc.rearrange("(b p t) -> p b t", b=NB, t=PACK))
+        nc.sync.dma_start(out=gain_sb[:], in_=gain.rearrange("(b p t) -> p b t", b=NB, t=PACK))
+        tabw = keep.tile([P, T], I32, name="tabw", tag="big_a", align_bytes=64)
+        nc.sync.dma_start(out=tabw[:], in_=tab_words[0].rearrange("p t i -> p (t i)").bitcast(I32))
+        for q in range(4):
+            nc.gpsimd.dma_start(out=w4s_raw[32 * q : 32 * q + 4, :].bitcast(I32), in_=w4_scales[0, 4 * q : 4 * q + 4, :].bitcast(I32))
+        for q in range(4):
+            nc.sync.dma_start(out=tabs[32 * q : 32 * q + 4, :].bitcast(I32), in_=tab_scales[0, 4 * q : 4 * q + 4, :].bitcast(I32))
+
+        def load_w(w, a, b):
+            raw = ring.tile([P, PACK, KP], F32, name="w_raw")
+            nc.sync.dma_start(out=raw[:], in_=w[a * KP : (a + 1) * KP, b * KP : (b + 1) * KP].rearrange("(p j) c -> p j c", j=PACK))
+            return raw
+
+        w1_raw = [load_w(w1, 0, 0)]
+
+        wgs_sb = keep.tile([P, PACK, S], F32, name="wgs_sb", tag="big_b", align_bytes=64)
+        wgs_rows = wgs.rearrange("(q t) c -> q t c", t=PACK)
+
+        def load_wgs(t0, t1):
+            for q in (0, 2, 1, 3):
+                nc.sync.dma_start(out=wgs_sb[32 * q : 32 * q + 32, t0:t1, :], in_=wgs_rows[:, t0:t1, :])
+
+        def load_light(s):
+            tl = ring.tile([P, S], F32, name="light", bufs=3)
+            nc.sync.dma_start(out=tl[:], in_=rows(light, s))
+            return tl
+
+        pages = [keep.tile([P, T2], F32, name="page%d" % s) for s in range(NS)]
+        lights = {0: load_light(0)}
+        load_wgs(0, 1)
+        nc.sync.dma_start(out=pages[0][:], in_=rows(page0, 0))
+        lights[1] = load_light(1)
+        load_wgs(1, PACK)
+        nc.sync.dma_start(out=pages[1][:], in_=rows(page0, 1))
+
+        w4d = keep.tile([P, 2 * H], U8, name="w4d", align_bytes=64)
+        w4sd = keep.tile([P, H], U8, name="w4sd", align_bytes=64)
+        nc.vector.tensor_copy(out=w4d[:].rearrange("p (b t m e) -> p b t m e", b=NB, t=PACK, e=2),
+                              in_=w4_raw[:].rearrange("p (b m t e) -> p b t m e", b=NB, t=PACK, e=2))
+        nc.vector.tensor_copy(out=w4sd[:].rearrange("p (b t m) -> p b t m", b=NB, t=PACK),
+                              in_=w4s_raw[:].rearrange("p (b m t) -> p b t m", b=NB, t=PACK))
+
+        vw = [keep.tile([P, HALF], I32, name="vw%d" % h, align_bytes=64) for h in range(2)]
+        vs = [keep.tile([P, HALF], U8, name="vs%d" % h, align_bytes=64) for h in range(2)]
+        for h in range(2):
+            nc.vector.tensor_copy(vw[h][:].bitcast(U32), tabw[:].bitcast(U32).indirect(l_tab[:, hoffs[h]]))
+            nc.vector.tensor_copy(vs[h][:], tabs[:].indirect(l_tab[:, hoffs[h]]))
+
+        w1c = [keep.tile([P, KP], I32, name="w1c%d" % b, align_bytes=64) for b in range(NB)]
+        w1s = [keep.tile([P, KP], U8, name="w1s%d" % b, align_bytes=64) for b in range(NB)]
+
+        def quant_w1(s):
+            b, t = divmod(s, PACK)
+            grouped = ring.tile([P, P, PACK], BF16, name="w1_bf", align_bytes=64)
+            nc.scalar.copy(out=grouped[:], in_=w1_raw[b][:].rearrange("p j (m t) -> p t m j", t=PACK)[:, t])
+            nc.vector.quantize_mx(out=w1c[b][:, t * P : (t + 1) * P].bitcast(FP8X4), scales=w1s[b][:, t * P : (t + 1) * P], in_=grouped[:].rearrange("p m j -> p (m j)"))
+
+        w2c = [[keep.tile([P, KP], I32, name="w2c%d%d" % (a, b), align_bytes=64) for b in range(NB)] for a in range(NB)]
+        w2s = [[keep.tile([P, KP], U8, name="w2s%d%d" % (a, b), align_bytes=64) for b in range(NB)] for a in range(NB)]
+
+        stage = [keep.tile([P, S], F32, name="stage%d" % i, align_bytes=64) for i in range(3)]
+
+        def cast_w2(raw, grouped):
+            nc.scalar.copy(out=grouped.rearrange("p (t m j) -> p m j t", t=PACK, j=PACK), in_=raw[:].rearrange("p j (m t) -> p m j t", t=PACK))
+
+        larger = [keep.tile([P, S], F32, name="larger%d" % i) for i in range(2)]
+        factor = [keep.tile([P, S], F32, name="factor%d" % i) for i in range(2)]
+        grain_ps = {}
+
+        def products(s):
+            b, t = divmod(s, PACK)
+            for h in range(2):
+                flaw = psum.tile([P, HALF], F32, name="acc")
+                nc.tensor.matmul_mx(out=flaw[:], lhsT=w4d[:, 2 * P * s : 2 * P * (s + 1)].bitcast(FP4X4), lhsT_scale=w4sd[:, P * s : P * (s + 1)],
+                                    rhs=vw[h][:].bitcast(FP8X4), rhs_scale=vs[h][:], start=True, stop=True)
+                grain = psum.tile([P, HALF], F32, name="acc")
+                nc.tensor.matmul_mx(out=grain[:], lhsT=w1c[b][:, t * P : (t + 1) * P].bitcast(FP8X4), lhsT_scale=w1s[b][:, t * P : (t + 1) * P],
+                                    rhs=vw[h][:].bitcast(FP8X4), rhs_scale=vs[h][:], start=True, stop=True)
+                nc.scalar.copy(out=stage[s % 3][:, hcols[h]], in_=flaw[:])
+                grain_ps[s, h] = grain
+
+        def make_factor(s):
+            nc.gpsimd.tensor_tensor(factor[s % 2][:], lights[s][:], wgs_sb[:, s % PACK, :], ALU.mult)
+
+        def take_larger(s):
+            for h in range(2):
+                nc.vector.tensor_tensor(larger[s % 2][:, hcols[h]], grain_ps[s, h][:], stage[s % 3][:, hcols[h]], ALU.max)
+
+        def put(s):
+            nc.vector.tensor_tensor(pages[s][:].indirect(l_put[:]), larger[s % 2][:], factor[s % 2][:], ALU.mult)
+
+        planes = {}
+
+        def squash(s, h, picked):
+            b, t = divmod(s, PACK)
+            if (b, h) not in planes:
+                planes[b, h] = ring.tile([P, PACK, HALF], BF16, name="planes", bufs=3, align_bytes=64)
+            sig = ring.tile([P, HALF], F32, name="sig")
+            nc.scalar.activation(sig[:], picked, ACT.Sigmoid, scale=sc_sb[:, b, t : t + 1])
+            nc.scalar.activation(planes[b, h][:, t, :], sig[:], ACT.Copy, scale=gain_sb[:, b, t : t + 1])
+
+        def pick(s, h, picked):
+            nc.vector.tensor_copy(picked, pages[s][:].indirect(l_dye[:, hoffs[h]]))
+
+        xc = [[keep.tile([P, HALF], I32, name="xc%d%d" % (b, h), align_bytes=64) for h in range(2)] for b in range(NB)]
+        xs = [[keep.tile([P, HALF], U8, name="xs%d%d" % (b, h), align_bytes=64) for h in range(2)] for b in range(NB)]
+
+        def weave_x(b, h, woven):
+            nc.scalar.copy(out=woven.rearrange("p (c i t) -> p c t i", i=4, t=PACK), in_=planes[b, h][:].rearrange("p t (c i) -> p c t i", i=4))
+
+        def quantise(codes, scales, values):
+            nc.vector.quantize_mx(out=codes[:].bitcast(FP8X4), scales=scales[:], in_=values)
+
+        for s in range(PACK):
+            quant_w1(s)
+        make_factor(0)
+        products(0)
+        take_larger(0)
+        for s in range(NS):
+            if s + 2 < NS:
+                lights[s + 2] = load_light(s + 2)
+                nc.sync.dma_start(out=pages[s + 2][:], in_=rows(page0, s + 2))
+            if s + 1 < NS:
+                make_factor(s + 1)
+                products(s + 1)
+            put(s)
+            if s + 1 < NS:
+                take_larger(s + 1)
+            spare = stage[s % 3][:].bitcast(BF16)
+            if s == 0:
+                cast_w2(load_w(w1, 0, 1), spare)
+                made = (w1c[1], w1s[1])
+            if 1 <= s <= 4:
+                a, b = divmod(s - 1, NB)
+                cast_w2(load_w(w2, a, b), spare)
+                made = (w2c[a][b], w2s[a][b])
+            if 5 <= s <= 6:
+                weave_x(0, s - 5, spare)
+                made = (xc[0][s - 5], xs[0][s - 5])
+            for h in range(2 if s < PACK else 1):
+                picked = ring.tile([P, HALF], F32, name="picked", bufs=3)
+                pick(s, h, picked[:])
+                squash(s, h, picked[:])
+            if s <= 6:
+                quantise(made[0], made[1], spare)
+        base_sb = [keep.tile([P, NB, PACK, HALF], F32, name="base%d" % h, tag=("big_a", "big_b")[h], align_bytes=64) for h in range(2)]
+        for h in range(2):
+            for b in range(NB):
+                nc.sync.dma_start(out=base_sb[h][:, b], in_=base.rearrange("(b p t) c -> b p t c", b=NB, t=PACK)[b][:, :, hcols[h]])
+        weave_x(1, 0, stage[1][:].bitcast(BF16))
+        quantise(xc[1][0], xs[1][0], stage[1][:].bitcast(BF16))
+        late = [larger[1][:, hcols[0]], larger[1][:, hcols[1]], factor[1][:, hcols[0]], factor[1][:, hcols[1]]]
+        for t in range(PACK):
+            pick(PACK + t, 1, late[t])
+        for t in range(PACK):
+            squash(PACK + t, 1, late[t])
+
+        def second(h, s):
+            b, t = divmod(s, PACK)
+            y = psum.tile([P, HALF], F32, name="acc")
+            for a in range(NB):
+                nc.tensor.matmul_mx(out=y[:], lhsT=w2c[a][b][:, t * P : (t + 1) * P].bitcast(FP8X4), lhsT_scale=w2s[a][b][:, t * P : (t + 1) * P],
+                                    rhs=xc[a][h][:].bitcast(FP8X4), rhs_scale=xs[a][h][:], start=(a == 0), stop=(a == NB - 1))
+            ysc = ring.tile([P, HALF], F32, name="ysc", bufs=3)
+            nc.scalar.activation(ysc[:], y[:], ACT.Copy, scale=sc_sb[:, b, t : t + 1])
+            prod = ring.tile([P, HALF], F32, name="picked", bufs=3)
+            nc.vector.tensor_tensor(prod[:], pages[s][:].indirect(l_herd[:, hoffs[h]]), ysc[:], ALU.mult)
+            return prod
+
+        def finish(h, s, prod):
+            b, t = divmod(s, PACK)
+            res = base_sb[h][:, b, t, :]
+            nc.vector.tensor_tensor(res, prod[:], res, ALU.add)
+            nc.sync.dma_start(out=rows(out, s)[:, hcols[h]], in_=res)
+
+        steps = [(h, s) for h in range(2) for s in range(NS)]
+        prev = None
+        for h, s in steps:
+            prod = second(h, s)
+            if prev is not None:
+                finish(*prev)
+            prev = (h, s, prod)
+            if (h, s) == (0, 1):
+                weave_x(1, 1, stage[2][:].bitcast(BF16))
+                quantise(xc[1][1], xs[1][1], stage[2][:].bitcast(BF16))
+        finish(*prev)

@@ -37,7 +37,7 @@ def tile_list_hide_grading_board_kernel(tc, tab_words, tab_scales, offs, w1, w4_
     with ExitStack() as ctx:
         keep = ctx.enter_context(tc.tile_pool(name="keep", bufs=1))
         ring = ctx.enter_context(tc.tile_pool(name="ring", bufs=2))
-        psum = ctx.enter_context(tc.psum_pool(name="psum", bufs=8))
+        psum = ctx.enter_context(tc.psum_pool(name="psum", bufs=2))
 
         l_tab = keep.tile([P, S // 16], U16, name="l_tab")
         l_put = keep.tile([P, S // 16], U16, name="l_put")
@@ -46,51 +46,44 @@ def tile_list_hide_grading_board_kernel(tc, tab_words, tab_scales, offs, w1, w4_
 
         w4s_raw = keep.tile([P, H], U8, name="w4s_raw", align_bytes=64)
         tabs = keep.tile([P, T], U8, name="tabs", align_bytes=64)
-        nc.vector.memset(w4s_raw[:].bitcast(I32), 0)
+        nc.gpsimd.memset(w4s_raw[:].bitcast(I32), 0)
         nc.vector.memset(tabs[:].bitcast(I32), 0)
         nc.sync.dma_start(l_tab[:], offs)
         w4_raw = keep.tile([P, 2 * H], U8, name="w4_raw", align_bytes=64)
         nc.sync.dma_start(out=w4_raw[:].bitcast(I32), in_=w4_words[0].bitcast(I32))
-        nc.sync.dma_start(l_put[:], offs2)
-        nc.sync.dma_start(l_dye[:], offs3)
-        nc.sync.dma_start(l_herd[:], offs4)
         sc_sb = keep.tile([P, NB, PACK], F32, name="sc_sb")
         gain_sb = keep.tile([P, NB, PACK], F32, name="gain_sb")
-        nc.sync.dma_start(out=sc_sb[:], in_=sc.rearrange("(b p t) -> p b t", b=NB, t=PACK))
-        nc.sync.dma_start(out=gain_sb[:], in_=gain.rearrange("(b p t) -> p b t", b=NB, t=PACK))
-        tabw = keep.tile([P, T], I32, name="tabw", tag="big_a", align_bytes=64)
-        nc.sync.dma_start(out=tabw[:], in_=tab_words[0].rearrange("p t i -> p (t i)").bitcast(I32))
-        for q in range(4):
-            nc.gpsimd.dma_start(out=w4s_raw[32 * q : 32 * q + 4, :].bitcast(I32), in_=w4_scales[0, 4 * q : 4 * q + 4, :].bitcast(I32))
-        for q in range(4):
-            nc.sync.dma_start(out=tabs[32 * q : 32 * q + 4, :].bitcast(I32), in_=tab_scales[0, 4 * q : 4 * q + 4, :].bitcast(I32))
 
         def load_w(w, a, b):
-            raw = ring.tile([P, PACK, KP], F32, name="w_raw")
+            raw = ring.tile([P, PACK, KP], F32, name="w_raw", bufs=3)
             nc.sync.dma_start(out=raw[:], in_=w[a * KP : (a + 1) * KP, b * KP : (b + 1) * KP].rearrange("(p j) c -> p j c", j=PACK))
             return raw
 
-        w1_raw = [load_w(w1, 0, 0)]
+        w1_first = load_w(w1, 0, 0)
+        tabw = keep.tile([P, T], I32, name="tabw", tag="big_a", align_bytes=64)
+        nc.sync.dma_start(out=tabw[:], in_=tab_words[0].rearrange("p t i -> p (t i)").bitcast(I32))
+        for q in range(4):
+            nc.scalar.dma_start(out=w4s_raw[32 * q : 32 * q + 4, :].bitcast(I32), in_=w4_scales[0, 4 * q : 4 * q + 4, :].bitcast(I32))
+        for q in range(4):
+            nc.gpsimd.dma_start(out=tabs[32 * q : 32 * q + 4, :].bitcast(I32), in_=tab_scales[0, 4 * q : 4 * q + 4, :].bitcast(I32))
 
         wgs_sb = keep.tile([P, PACK, S], F32, name="wgs_sb", tag="big_b", align_bytes=64)
         wgs_rows = wgs.rearrange("(q t) c -> q t c", t=PACK)
 
-        def load_wgs(t0, t1):
+        def load_wgs(t):
             for q in (0, 2, 1, 3):
-                nc.sync.dma_start(out=wgs_sb[32 * q : 32 * q + 32, t0:t1, :], in_=wgs_rows[:, t0:t1, :])
+                nc.sync.dma_start(out=wgs_sb[32 * q : 32 * q + 32, t, :], in_=wgs_rows[:, t, :])
 
         def load_light(s):
-            tl = ring.tile([P, S], F32, name="light", bufs=3)
-            nc.sync.dma_start(out=tl[:], in_=rows(light, s))
-            return tl
+            nc.sync.dma_start(out=factor[s][:], in_=rows(light, s))
 
         pages = [keep.tile([P, T2], F32, name="page%d" % s) for s in range(NS)]
-        lights = {0: load_light(0)}
-        load_wgs(0, 1)
+        factor = [keep.tile([P, S], F32, name="factor%d" % s) for s in range(NS)]
+        load_light(0)
+        load_wgs(0)
+        nc.sync.dma_start(l_put[:], offs2)
         nc.sync.dma_start(out=pages[0][:], in_=rows(page0, 0))
-        lights[1] = load_light(1)
-        load_wgs(1, PACK)
-        nc.sync.dma_start(out=pages[1][:], in_=rows(page0, 1))
+        nc.sync.dma_start(l_dye[:], offs3)
 
         w4d = keep.tile([P, 2 * H], U8, name="w4d", align_bytes=64)
         w4sd = keep.tile([P, H], U8, name="w4sd", align_bytes=64)
@@ -106,54 +99,53 @@ def tile_list_hide_grading_board_kernel(tc, tab_words, tab_scales, offs, w1, w4_
             nc.vector.tensor_copy(vs[h][:], tabs[:].indirect(l_tab[:, hoffs[h]]))
 
         w1c = [keep.tile([P, KP], I32, name="w1c%d" % b, align_bytes=64) for b in range(NB)]
-        w1s = [keep.tile([P, KP], U8, name="w1s%d" % b, align_bytes=64) for b in range(NB)]
+        shared = keep.tile([P, 9 * P], U8, name="shared", align_bytes=64)
 
-        def quant_w1(s):
-            b, t = divmod(s, PACK)
-            grouped = ring.tile([P, P, PACK], BF16, name="w1_bf", align_bytes=64)
-            nc.scalar.copy(out=grouped[:], in_=w1_raw[b][:].rearrange("p j (m t) -> p t m j", t=PACK)[:, t])
-            nc.vector.quantize_mx(out=w1c[b][:, t * P : (t + 1) * P].bitcast(FP8X4), scales=w1s[b][:, t * P : (t + 1) * P], in_=grouped[:].rearrange("p m j -> p (m j)"))
+        def plane(row, col):
+            return shared[row:P, col * P : col * P + KP]
+
+        w1s = [plane(0, 1), plane(4, 3)]
 
         w2c = [[keep.tile([P, KP], I32, name="w2c%d%d" % (a, b), align_bytes=64) for b in range(NB)] for a in range(NB)]
-        w2s = [[keep.tile([P, KP], U8, name="w2s%d%d" % (a, b), align_bytes=64) for b in range(NB)] for a in range(NB)]
+        w2s = [[plane(8, 4), plane(8, 0)], [plane(12, 1), plane(12, 5)]]
 
         stage = [keep.tile([P, S], F32, name="stage%d" % i, align_bytes=64) for i in range(3)]
 
         def cast_w2(raw, grouped):
             nc.scalar.copy(out=grouped.rearrange("p (t m j) -> p m j t", t=PACK, j=PACK), in_=raw[:].rearrange("p j (m t) -> p m j t", t=PACK))
 
-        larger = [keep.tile([P, S], F32, name="larger%d" % i) for i in range(2)]
-        factor = [keep.tile([P, S], F32, name="factor%d" % i) for i in range(2)]
+        larger = keep.tile([P, S], F32, name="larger")
+        scaled = keep.tile([P, S], F32, name="scaled")
         grain_ps = {}
 
         def products(s):
             b, t = divmod(s, PACK)
             for h in range(2):
-                flaw = psum.tile([P, HALF], F32, name="acc")
+                flaw = psum.tile([P, HALF], F32, name="flaw")
                 nc.tensor.matmul_mx(out=flaw[:], lhsT=w4d[:, 2 * P * s : 2 * P * (s + 1)].bitcast(FP4X4), lhsT_scale=w4sd[:, P * s : P * (s + 1)],
                                     rhs=vw[h][:].bitcast(FP8X4), rhs_scale=vs[h][:], start=True, stop=True)
-                grain = psum.tile([P, HALF], F32, name="acc")
+                grain = psum.tile([P, HALF], F32, name="grain")
                 nc.tensor.matmul_mx(out=grain[:], lhsT=w1c[b][:, t * P : (t + 1) * P].bitcast(FP8X4), lhsT_scale=w1s[b][:, t * P : (t + 1) * P],
                                     rhs=vw[h][:].bitcast(FP8X4), rhs_scale=vs[h][:], start=True, stop=True)
                 nc.scalar.copy(out=stage[s % 3][:, hcols[h]], in_=flaw[:])
                 grain_ps[s, h] = grain
 
-        def make_factor(s):
-            nc.gpsimd.tensor_tensor(factor[s % 2][:], lights[s][:], wgs_sb[:, s % PACK, :], ALU.mult)
+        def make_factor(s, engine):
+            engine.tensor_tensor(scaled[:], factor[s][:], wgs_sb[:, s % PACK, :], ALU.mult)
 
         def take_larger(s):
             for h in range(2):
-                nc.vector.tensor_tensor(larger[s % 2][:, hcols[h]], grain_ps[s, h][:], stage[s % 3][:, hcols[h]], ALU.max)
+                nc.vector.tensor_tensor(larger[:, hcols[h]], grain_ps[s, h][:], stage[s % 3][:, hcols[h]], ALU.max)
 
         def put(s):
-            nc.vector.tensor_tensor(pages[s][:].indirect(l_put[:]), larger[s % 2][:], factor[s % 2][:], ALU.mult)
+            nc.vector.tensor_tensor(pages[s][:].indirect(l_put[:]), larger[:], scaled[:], ALU.mult)
 
         planes = {}
 
         def squash(s, h, picked):
             b, t = divmod(s, PACK)
             if (b, h) not in planes:
-                planes[b, h] = ring.tile([P, PACK, HALF], BF16, name="planes", bufs=3, align_bytes=64)
+                planes[b, h] = ring.tile([P, PACK, HALF], BF16, name="planes", bufs=4, align_bytes=64)
             sig = ring.tile([P, HALF], F32, name="sig")
             nc.scalar.activation(sig[:], picked, ACT.Sigmoid, scale=sc_sb[:, b, t : t + 1])
             nc.scalar.activation(planes[b, h][:, t, :], sig[:], ACT.Copy, scale=gain_sb[:, b, t : t + 1])
@@ -162,84 +154,107 @@ def tile_list_hide_grading_board_kernel(tc, tab_words, tab_scales, offs, w1, w4_
             nc.vector.tensor_copy(picked, pages[s][:].indirect(l_dye[:, hoffs[h]]))
 
         xc = [[keep.tile([P, HALF], I32, name="xc%d%d" % (b, h), align_bytes=64) for h in range(2)] for b in range(NB)]
-        xs = [[keep.tile([P, HALF], U8, name="xs%d%d" % (b, h), align_bytes=64) for h in range(2)] for b in range(NB)]
+        xs_own = [keep.tile([P, HALF], U8, name="xs%d" % i, align_bytes=64) for i in range(3)]
+        xs = [[plane(0, 5), xs_own[0][:]], [xs_own[1][:], xs_own[2][:]]]
 
-        def weave_x(b, h, woven):
-            nc.scalar.copy(out=woven.rearrange("p (c i t) -> p c t i", i=4, t=PACK), in_=planes[b, h][:].rearrange("p t (c i) -> p c t i", i=4))
+        def weave_x(b, h, woven, copy, c0, c1):
+            copy(out=woven[:, PACK * c0 : PACK * c1].rearrange("p (c i t) -> p c t i", i=4, t=PACK),
+                 in_=planes[b, h][:, :, c0:c1].rearrange("p t (c i) -> p c t i", i=4))
 
         def quantise(codes, scales, values):
-            nc.vector.quantize_mx(out=codes[:].bitcast(FP8X4), scales=scales[:], in_=values)
+            nc.vector.quantize_mx(out=codes[:].bitcast(FP8X4), scales=scales, in_=values)
 
-        for s in range(PACK):
-            quant_w1(s)
-        make_factor(0)
+        weights = {0: (w1, 0, 1, w1c[1], w1s[1])}
+        for i in range(NB * NB):
+            a, b = divmod(i, NB)
+            weights[1 + i] = (w2, a, b, w2c[a][b], w2s[a][b])
+        raws = {}
+
+        def load_slice(s):
+            load_light(s)
+            if s < PACK:
+                load_wgs(s)
+            if s in weights:
+                raws[s] = load_w(*weights[s][:3])
+            nc.sync.dma_start(out=pages[s][:], in_=rows(page0, s))
+
+        raws[0] = load_w(*weights[0][:3])
+        load_slice(1)
+        nc.sync.dma_start(out=sc_sb[:], in_=sc.rearrange("(b p t) -> p b t", b=NB, t=PACK))
+        nc.sync.dma_start(out=gain_sb[:], in_=gain.rearrange("(b p t) -> p b t", b=NB, t=PACK))
+        nc.sync.dma_start(l_herd[:], offs4)
+
+        cast_w2(w1_first, stage[2][:].bitcast(BF16))
+        quantise(w1c[0], w1s[0], stage[2][:].bitcast(BF16))
         products(0)
+        make_factor(0, nc.vector)
         take_larger(0)
+        products(1)
         for s in range(NS):
             if s + 2 < NS:
-                lights[s + 2] = load_light(s + 2)
-                nc.sync.dma_start(out=pages[s + 2][:], in_=rows(page0, s + 2))
-            if s + 1 < NS:
-                make_factor(s + 1)
-                products(s + 1)
+                load_slice(s + 2)
+            spare = stage[s % 3][:].bitcast(BF16)
+            if s in raws:
+                cast_w2(raws[s], spare)
+                made = weights[s][3:]
+            elif s + 1 < NS:
+                h = s - len(weights)
+                weave_x(0, h, spare, nc.scalar.copy, 0, HALF)
+                made = (xc[0][h], xs[0][h])
+            if s >= 1:
+                for h in range(2 if s - 1 < PACK else 1):
+                    squash(s - 1, h, factor[s - 1][:, hcols[h]])
             put(s)
             if s + 1 < NS:
                 take_larger(s + 1)
-            spare = stage[s % 3][:].bitcast(BF16)
-            if s == 0:
-                cast_w2(load_w(w1, 0, 1), spare)
-                made = (w1c[1], w1s[1])
-            if 1 <= s <= 4:
-                a, b = divmod(s - 1, NB)
-                cast_w2(load_w(w2, a, b), spare)
-                made = (w2c[a][b], w2s[a][b])
-            if 5 <= s <= 6:
-                weave_x(0, s - 5, spare)
-                made = (xc[0][s - 5], xs[0][s - 5])
-            for h in range(2 if s < PACK else 1):
-                picked = ring.tile([P, HALF], F32, name="picked", bufs=3)
-                pick(s, h, picked[:])
-                squash(s, h, picked[:])
-            if s <= 6:
+                make_factor(s + 1, nc.gpsimd)
+            if s + 2 < NS:
+                products(s + 2)
+            if s < PACK:
+                nc.vector.tensor_copy(factor[s][:], pages[s][:].indirect(l_dye[:]))
+            else:
+                pick(s, 0, factor[s][:, hcols[0]])
+            if s + 1 < NS:
                 quantise(made[0], made[1], spare)
         base_sb = [keep.tile([P, NB, PACK, HALF], F32, name="base%d" % h, tag=("big_a", "big_b")[h], align_bytes=64) for h in range(2)]
         for h in range(2):
             for b in range(NB):
                 nc.sync.dma_start(out=base_sb[h][:, b], in_=base.rearrange("(b p t) c -> b p t c", b=NB, t=PACK)[b][:, :, hcols[h]])
-        weave_x(1, 0, stage[1][:].bitcast(BF16))
-        quantise(xc[1][0], xs[1][0], stage[1][:].bitcast(BF16))
-        late = [larger[1][:, hcols[0]], larger[1][:, hcols[1]], factor[1][:, hcols[0]], factor[1][:, hcols[1]]]
+        squash(NS - 1, 0, factor[NS - 1][:, hcols[0]])
+        late = [larger[:, hcols[0]], larger[:, hcols[1]], scaled[:, hcols[0]], scaled[:, hcols[1]]]
         for t in range(PACK):
             pick(PACK + t, 1, late[t])
-        for t in range(PACK):
-            squash(PACK + t, 1, late[t])
-
-        def second(h, s):
-            b, t = divmod(s, PACK)
-            y = psum.tile([P, HALF], F32, name="acc")
-            for a in range(NB):
-                nc.tensor.matmul_mx(out=y[:], lhsT=w2c[a][b][:, t * P : (t + 1) * P].bitcast(FP8X4), lhsT_scale=w2s[a][b][:, t * P : (t + 1) * P],
-                                    rhs=xc[a][h][:].bitcast(FP8X4), rhs_scale=xs[a][h][:], start=(a == 0), stop=(a == NB - 1))
-            ysc = ring.tile([P, HALF], F32, name="ysc", bufs=3)
-            nc.scalar.activation(ysc[:], y[:], ACT.Copy, scale=sc_sb[:, b, t : t + 1])
-            prod = ring.tile([P, HALF], F32, name="picked", bufs=3)
-            nc.vector.tensor_tensor(prod[:], pages[s][:].indirect(l_herd[:, hoffs[h]]), ysc[:], ALU.mult)
-            return prod
-
-        def finish(h, s, prod):
-            b, t = divmod(s, PACK)
-            res = base_sb[h][:, b, t, :]
-            nc.vector.tensor_tensor(res, prod[:], res, ALU.add)
-            nc.sync.dma_start(out=rows(out, s)[:, hcols[h]], in_=res)
+        weave_x(1, 0, stage[1][:].bitcast(BF16), nc.scalar.copy, 0, HALF // 2)
+        weave_x(1, 0, stage[1][:].bitcast(BF16), nc.vector.tensor_copy, HALF // 2, HALF)
+        quantise(xc[1][0], xs[1][0], stage[1][:].bitcast(BF16))
 
         steps = [(h, s) for h in range(2) for s in range(NS)]
-        prev = None
-        for h, s in steps:
-            prod = second(h, s)
-            if prev is not None:
-                finish(*prev)
-            prev = (h, s, prod)
-            if (h, s) == (0, 1):
-                weave_x(1, 1, stage[2][:].bitcast(BF16))
+
+        def multiply(i):
+            h, s = steps[i]
+            b, t = divmod(s, PACK)
+            y = psum.tile([P, HALF], F32, name="y", bufs=4)
+            for a in range(NB):
+                nc.tensor.matmul_mx(out=y[:], lhsT=w2c[a][b][:, t * P : (t + 1) * P].bitcast(FP8X4), lhsT_scale=w2s[a][b][:, t * P : (t + 1) * P],
+                                    rhs=xc[a][h][:].bitcast(FP8X4), rhs_scale=xs[a][h], start=(a == 0), stop=(a == NB - 1))
+            ysc = factor[i // 2 % 2][:, hcols[i % 2]]
+            nc.scalar.activation(ysc, y[:], ACT.Copy, scale=sc_sb[:, b, t : t + 1])
+            nc.vector.tensor_tensor(factor[2][:, hcols[i % 2]], pages[s][:].indirect(l_herd[:, hoffs[h]]), ysc, ALU.mult)
+
+        def finish(i):
+            h, s = steps[i]
+            res = base_sb[h][:, s // PACK, s % PACK, :]
+            nc.vector.tensor_tensor(res, factor[2][:, hcols[i % 2]], res, ALU.add)
+            nc.sync.dma_start(out=rows(out, s)[:, hcols[h]], in_=res)
+
+        n = len(steps)
+        for i in range(n + 1):
+            if i < n:
+                multiply(i)
+            if i >= 1:
+                finish(i - 1)
+            if i < PACK:
+                squash(PACK + i, 1, late[i])
+            if i == PACK:
+                weave_x(1, 1, stage[2][:].bitcast(BF16), nc.scalar.copy, 0, HALF)
                 quantise(xc[1][1], xs[1][1], stage[2][:].bitcast(BF16))
-        finish(*prev)

@@ -1,6 +1,7 @@
 from contextlib import ExitStack
 
 import concourse.mybir as mybir
+from concourse.masks import make_identity
 
 K, H, T, S, T2, NP = 512, 1024, 4096, 1024, 2048, 1024
 FLOPS = 2 * (2 * K * H * S + H * H * NP)
@@ -22,13 +23,15 @@ KP = P * PACK
 HALF = 512
 NB = H // KP
 NS = NB * PACK
+QUADS = 4
+STAGES = 3
 
 
 def tile_list_hide_grading_board_kernel(tc, tab_words, tab_scales, offs, w1, w4_words, w4_scales, light, page0,
                                                  wgs, offs2, sc, offs3, gain, w2, offs4, base, out):
     nc = tc.nc
-    hcols = [slice(h * HALF, (h + 1) * HALF) for h in range(2)]
-    hoffs = [slice(h * HALF // 16, (h + 1) * HALF // 16) for h in range(2)]
+    cols = [slice(h * HALF, (h + 1) * HALF) for h in range(2)]
+    entries = [slice(h * HALF // 16, (h + 1) * HALF // 16) for h in range(2)]
 
     def rows(ap, s):
         b, t = divmod(s, PACK)
@@ -62,9 +65,9 @@ def tile_list_hide_grading_board_kernel(tc, tab_words, tab_scales, offs, w1, w4_
         w1_first = load_w(w1, 0, 0)
         tabw = keep.tile([P, T], I32, name="tabw", tag="big_a", align_bytes=64)
         nc.sync.dma_start(out=tabw[:], in_=tab_words[0].rearrange("p t i -> p (t i)").bitcast(I32))
-        for q in range(4):
+        for q in range(QUADS):
             nc.scalar.dma_start(out=w4s_raw[32 * q : 32 * q + 4, :].bitcast(I32), in_=w4_scales[0, 4 * q : 4 * q + 4, :].bitcast(I32))
-        for q in range(4):
+        for q in range(QUADS):
             nc.gpsimd.dma_start(out=tabs[32 * q : 32 * q + 4, :].bitcast(I32), in_=tab_scales[0, 4 * q : 4 * q + 4, :].bitcast(I32))
 
         wgs_sb = keep.tile([P, PACK, S], F32, name="wgs_sb", tag="big_b", align_bytes=64)
@@ -75,10 +78,10 @@ def tile_list_hide_grading_board_kernel(tc, tab_words, tab_scales, offs, w1, w4_
                 nc.sync.dma_start(out=wgs_sb[32 * q : 32 * q + 32, t, :], in_=wgs_rows[:, t, :])
 
         def load_light(s):
-            nc.sync.dma_start(out=factor[s][:], in_=rows(light, s))
+            nc.sync.dma_start(out=work[s][:], in_=rows(light, s))
 
         pages = [keep.tile([P, T2], F32, name="page%d" % s) for s in range(NS)]
-        factor = [keep.tile([P, S], F32, name="factor%d" % s) for s in range(NS)]
+        work = [keep.tile([P, S], F32, name="work%d" % s) for s in range(NS)]
         load_light(0)
         load_wgs(0)
         nc.sync.dma_start(l_put[:], offs2)
@@ -92,11 +95,14 @@ def tile_list_hide_grading_board_kernel(tc, tab_words, tab_scales, offs, w1, w4_
         nc.vector.tensor_copy(out=w4sd[:].rearrange("p (b t m) -> p b t m", b=NB, t=PACK),
                               in_=w4s_raw[:].rearrange("p (b m t) -> p b t m", b=NB, t=PACK))
 
+        ident = keep.tile([P, P], F32, name="ident")
+        make_identity(nc, ident[:])
+
         vw = [keep.tile([P, HALF], I32, name="vw%d" % h, align_bytes=64) for h in range(2)]
         vs = [keep.tile([P, HALF], U8, name="vs%d" % h, align_bytes=64) for h in range(2)]
         for h in range(2):
-            nc.vector.tensor_copy(vw[h][:].bitcast(U32), tabw[:].bitcast(U32).indirect(l_tab[:, hoffs[h]]))
-            nc.vector.tensor_copy(vs[h][:], tabs[:].indirect(l_tab[:, hoffs[h]]))
+            nc.vector.tensor_copy(vw[h][:].bitcast(U32), tabw[:].bitcast(U32).indirect(l_tab[:, entries[h]]))
+            nc.vector.tensor_copy(vs[h][:], tabs[:].indirect(l_tab[:, entries[h]]))
 
         w1c = [keep.tile([P, KP], I32, name="w1c%d" % b, align_bytes=64) for b in range(NB)]
         shared = keep.tile([P, 9 * P], U8, name="shared", align_bytes=64)
@@ -109,9 +115,9 @@ def tile_list_hide_grading_board_kernel(tc, tab_words, tab_scales, offs, w1, w4_
         w2c = [[keep.tile([P, KP], I32, name="w2c%d%d" % (a, b), align_bytes=64) for b in range(NB)] for a in range(NB)]
         w2s = [[plane(8, 4), plane(8, 0)], [plane(12, 1), plane(12, 5)]]
 
-        stage = [keep.tile([P, S], F32, name="stage%d" % i, align_bytes=64) for i in range(3)]
+        stage = [keep.tile([P, S], F32, name="stage%d" % i, align_bytes=64) for i in range(STAGES)]
 
-        def cast_w2(raw, grouped):
+        def cast_w(raw, grouped):
             nc.scalar.copy(out=grouped.rearrange("p (t m j) -> p m j t", t=PACK, j=PACK), in_=raw[:].rearrange("p j (m t) -> p m j t", t=PACK))
 
         larger = keep.tile([P, S], F32, name="larger")
@@ -121,45 +127,45 @@ def tile_list_hide_grading_board_kernel(tc, tab_words, tab_scales, offs, w1, w4_
         def products(s):
             b, t = divmod(s, PACK)
             for h in range(2):
-                flaw = psum.tile([P, HALF], F32, name="flaw")
+                flaw = psum.tile([P, HALF], F32, name="bank_a")
                 nc.tensor.matmul_mx(out=flaw[:], lhsT=w4d[:, 2 * P * s : 2 * P * (s + 1)].bitcast(FP4X4), lhsT_scale=w4sd[:, P * s : P * (s + 1)],
                                     rhs=vw[h][:].bitcast(FP8X4), rhs_scale=vs[h][:], start=True, stop=True)
-                grain = psum.tile([P, HALF], F32, name="grain")
+                grain = psum.tile([P, HALF], F32, name="bank_b")
                 nc.tensor.matmul_mx(out=grain[:], lhsT=w1c[b][:, t * P : (t + 1) * P].bitcast(FP8X4), lhsT_scale=w1s[b][:, t * P : (t + 1) * P],
                                     rhs=vw[h][:].bitcast(FP8X4), rhs_scale=vs[h][:], start=True, stop=True)
-                nc.scalar.copy(out=stage[s % 3][:, hcols[h]], in_=flaw[:])
+                nc.scalar.copy(out=stage[s % STAGES][:, cols[h]], in_=flaw[:])
                 grain_ps[s, h] = grain
 
-        def make_factor(s, engine):
-            engine.tensor_tensor(scaled[:], factor[s][:], wgs_sb[:, s % PACK, :], ALU.mult)
+        def scale_light(s, engine):
+            engine.tensor_tensor(scaled[:], work[s][:], wgs_sb[:, s % PACK, :], ALU.mult)
 
         def take_larger(s):
             for h in range(2):
-                nc.vector.tensor_tensor(larger[:, hcols[h]], grain_ps[s, h][:], stage[s % 3][:, hcols[h]], ALU.max)
+                nc.vector.tensor_tensor(larger[:, cols[h]], grain_ps[s, h][:], stage[s % STAGES][:, cols[h]], ALU.max)
 
         def put(s):
             nc.vector.tensor_tensor(pages[s][:].indirect(l_put[:]), larger[:], scaled[:], ALU.mult)
 
-        planes = {}
+        quarters = {}
 
         def squash(s, h, picked):
             b, t = divmod(s, PACK)
-            if (b, h) not in planes:
-                planes[b, h] = ring.tile([P, PACK, HALF], BF16, name="planes", bufs=4, align_bytes=64)
+            if (b, h) not in quarters:
+                quarters[b, h] = ring.tile([P, PACK, HALF], BF16, name="quarter", bufs=NB * 2, align_bytes=64)
             sig = ring.tile([P, HALF], F32, name="sig")
             nc.scalar.activation(sig[:], picked, ACT.Sigmoid, scale=sc_sb[:, b, t : t + 1])
-            nc.scalar.activation(planes[b, h][:, t, :], sig[:], ACT.Copy, scale=gain_sb[:, b, t : t + 1])
+            nc.scalar.activation(quarters[b, h][:, t, :], sig[:], ACT.Copy, scale=gain_sb[:, b, t : t + 1])
 
         def pick(s, h, picked):
-            nc.vector.tensor_copy(picked, pages[s][:].indirect(l_dye[:, hoffs[h]]))
+            nc.vector.tensor_copy(picked, pages[s][:].indirect(l_dye[:, entries[h]]))
 
         xc = [[keep.tile([P, HALF], I32, name="xc%d%d" % (b, h), align_bytes=64) for h in range(2)] for b in range(NB)]
-        xs_own = [keep.tile([P, HALF], U8, name="xs%d" % i, align_bytes=64) for i in range(3)]
+        xs_own = [keep.tile([P, HALF], U8, name="xs%d" % i, align_bytes=64) for i in range(NB * 2 - 1)]
         xs = [[plane(0, 5), xs_own[0][:]], [xs_own[1][:], xs_own[2][:]]]
 
         def weave_x(b, h, woven, copy, c0, c1):
             copy(out=woven[:, PACK * c0 : PACK * c1].rearrange("p (c i t) -> p c t i", i=4, t=PACK),
-                 in_=planes[b, h][:, :, c0:c1].rearrange("p t (c i) -> p c t i", i=4))
+                 in_=quarters[b, h][:, :, c0:c1].rearrange("p t (c i) -> p c t i", i=4))
 
         def quantise(codes, scales, values):
             nc.vector.quantize_mx(out=codes[:].bitcast(FP8X4), scales=scales, in_=values)
@@ -184,18 +190,19 @@ def tile_list_hide_grading_board_kernel(tc, tab_words, tab_scales, offs, w1, w4_
         nc.sync.dma_start(out=gain_sb[:], in_=gain.rearrange("(b p t) -> p b t", b=NB, t=PACK))
         nc.sync.dma_start(l_herd[:], offs4)
 
-        cast_w2(w1_first, stage[2][:].bitcast(BF16))
-        quantise(w1c[0], w1s[0], stage[2][:].bitcast(BF16))
+        first_in = stage[STAGES - 1][:].bitcast(BF16)
+        cast_w(w1_first, first_in)
+        quantise(w1c[0], w1s[0], first_in)
         products(0)
-        make_factor(0, nc.vector)
+        scale_light(0, nc.vector)
         take_larger(0)
         products(1)
         for s in range(NS):
             if s + 2 < NS:
                 load_slice(s + 2)
-            spare = stage[s % 3][:].bitcast(BF16)
+            spare = stage[s % STAGES][:].bitcast(BF16)
             if s in raws:
-                cast_w2(raws[s], spare)
+                cast_w(raws[s], spare)
                 made = weights[s][3:]
             elif s + 1 < NS:
                 h = s - len(weights)
@@ -203,32 +210,40 @@ def tile_list_hide_grading_board_kernel(tc, tab_words, tab_scales, offs, w1, w4_
                 made = (xc[0][h], xs[0][h])
             if s >= 1:
                 for h in range(2 if s - 1 < PACK else 1):
-                    squash(s - 1, h, factor[s - 1][:, hcols[h]])
+                    squash(s - 1, h, work[s - 1][:, cols[h]])
             put(s)
             if s + 1 < NS:
                 take_larger(s + 1)
-                make_factor(s + 1, nc.gpsimd)
+                scale_light(s + 1, nc.gpsimd)
             if s + 2 < NS:
                 products(s + 2)
             if s < PACK:
-                nc.vector.tensor_copy(factor[s][:], pages[s][:].indirect(l_dye[:]))
+                nc.vector.tensor_copy(work[s][:], pages[s][:].indirect(l_dye[:]))
             else:
-                pick(s, 0, factor[s][:, hcols[0]])
+                pick(s, 0, work[s][:, cols[0]])
             if s + 1 < NS:
                 quantise(made[0], made[1], spare)
+
         base_sb = [keep.tile([P, NB, PACK, HALF], F32, name="base%d" % h, tag=("big_a", "big_b")[h], align_bytes=64) for h in range(2)]
         for h in range(2):
             for b in range(NB):
-                nc.sync.dma_start(out=base_sb[h][:, b], in_=base.rearrange("(b p t) c -> b p t c", b=NB, t=PACK)[b][:, :, hcols[h]])
-        squash(NS - 1, 0, factor[NS - 1][:, hcols[0]])
-        late = [larger[:, hcols[0]], larger[:, hcols[1]], scaled[:, hcols[0]], scaled[:, hcols[1]]]
-        for t in range(PACK):
+                nc.sync.dma_start(out=base_sb[h][:, b], in_=base.rearrange("(b p t) c -> b p t c", b=NB, t=PACK)[b][:, :, cols[h]])
+
+        last_stage = stage[(NS - 1) % STAGES]
+        squash(NS - 1, 0, work[NS - 1][:, cols[0]])
+        late = [larger[:, cols[0]], larger[:, cols[1]], last_stage[:, cols[0]], last_stage[:, cols[1]]]
+        for t in range(PACK // 2):
             pick(PACK + t, 1, late[t])
-        weave_x(1, 0, stage[1][:].bitcast(BF16), nc.scalar.copy, 0, HALF // 2)
-        weave_x(1, 0, stage[1][:].bitcast(BF16), nc.vector.tensor_copy, HALF // 2, HALF)
-        quantise(xc[1][0], xs[1][0], stage[1][:].bitcast(BF16))
+        weave_x(1, 0, last_stage[:].bitcast(BF16), nc.scalar.copy, 0, HALF // 2)
+        weave_x(1, 0, last_stage[:].bitcast(BF16), nc.vector.tensor_copy, HALF // 2, HALF)
+        quantise(xc[1][0], xs[1][0], last_stage[:].bitcast(BF16))
+        for t in range(PACK // 2, PACK):
+            pick(PACK + t, 1, late[t])
 
         steps = [(h, s) for h in range(2) for s in range(NS)]
+
+        def buffer_of(i, first, tiles):
+            return work[first + i // 2 % tiles][:, cols[i % 2]]
 
         def multiply(i):
             h, s = steps[i]
@@ -237,24 +252,55 @@ def tile_list_hide_grading_board_kernel(tc, tab_words, tab_scales, offs, w1, w4_
             for a in range(NB):
                 nc.tensor.matmul_mx(out=y[:], lhsT=w2c[a][b][:, t * P : (t + 1) * P].bitcast(FP8X4), lhsT_scale=w2s[a][b][:, t * P : (t + 1) * P],
                                     rhs=xc[a][h][:].bitcast(FP8X4), rhs_scale=xs[a][h], start=(a == 0), stop=(a == NB - 1))
-            ysc = factor[i // 2 % 2][:, hcols[i % 2]]
+            ysc = buffer_of(i, 0, 2)
             nc.scalar.activation(ysc, y[:], ACT.Copy, scale=sc_sb[:, b, t : t + 1])
-            nc.vector.tensor_tensor(factor[2][:, hcols[i % 2]], pages[s][:].indirect(l_herd[:, hoffs[h]]), ysc, ALU.mult)
+            nc.vector.tensor_tensor(product(i), pages[s][:].indirect(l_herd[:, entries[h]]), ysc, ALU.mult)
 
-        def finish(i):
+        def product(i):
+            return buffer_of(i, 2, 2)
+
+        def turned_sum(i):
+            return buffer_of(i // 2, 4, 1)
+
+        def base_of(i):
             h, s = steps[i]
-            res = base_sb[h][:, s // PACK, s % PACK, :]
-            nc.vector.tensor_tensor(res, factor[2][:, hcols[i % 2]], res, ALU.add)
-            nc.sync.dma_start(out=rows(out, s)[:, hcols[h]], in_=res)
+            return base_sb[h][:, s // PACK, s % PACK, :]
+
+        def store(i):
+            h, s = steps[i]
+            nc.sync.dma_start(out=rows(out, s)[:, cols[h]], in_=base_of(i))
+
+        squares = [slice(c * P, (c + 1) * P) for c in range(HALF // P)]
+
+        def add_turned(i):
+            turned = psum.tile([P, HALF], F32, name="bank_a")
+            for sq in squares:
+                nc.tensor.matmul(turned[:, sq], base_of(i)[:, sq], ident[:], start=True, stop=False, is_transpose=True)
+                nc.tensor.matmul(turned[:, sq], product(i)[:, sq], ident[:], start=False, stop=True, is_transpose=True)
+            nc.scalar.copy(out=turned_sum(i), in_=turned[:])
+
+        def turn_back(i):
+            back = psum.tile([P, HALF], F32, name="bank_b")
+            for sq in squares:
+                nc.tensor.transpose(back[:, sq], turned_sum(i)[:, sq], ident[:])
+            nc.scalar.copy(out=base_of(i), in_=back[:])
+            store(i)
 
         n = len(steps)
+        on_tensor = range(PACK + 1, n - 2, 2)
         for i in range(n + 1):
             if i < n:
                 multiply(i)
-            if i >= 1:
-                finish(i - 1)
+            if i >= 1 and i - 1 not in on_tensor:
+                nc.vector.tensor_tensor(base_of(i - 1), product(i - 1), base_of(i - 1), ALU.add)
+                store(i - 1)
+            if i - 2 in on_tensor:
+                add_turned(i - 2)
+            if i - 3 in on_tensor:
+                turn_back(i - 3)
             if i < PACK:
                 squash(PACK + i, 1, late[i])
             if i == PACK:
-                weave_x(1, 1, stage[2][:].bitcast(BF16), nc.scalar.copy, 0, HALF)
-                quantise(xc[1][1], xs[1][1], stage[2][:].bitcast(BF16))
+                last_in = stage[NS % STAGES][:].bitcast(BF16)
+                weave_x(1, 1, last_in, nc.scalar.copy, 0, HALF)
+                quantise(xc[1][1], xs[1][1], last_in)

from contextlib import ExitStack

import concourse.mybir as mybir
from concourse.masks import make_identity

K, H, T, S, T2, NP = 512, 1024, 4096, 1024, 2048, 1024
FLOPS = 2 * (2 * K * H * S + H * H * NP)

F32 = mybir.dt.float32
BF16 = mybir.dt.bfloat16
I32 = mybir.dt.int32
U32 = mybir.dt.uint32
U16 = mybir.dt.uint16
U8 = mybir.dt.uint8
FP8X4 = mybir.dt.float8_e4m3fn_x4
FP4X4 = mybir.dt.float4_e2m1fn_x4
ACT = mybir.ActivationFunctionType
ALU = mybir.AluOpType

P = 128
PACK = 4
KP = P * PACK
HALF = 512
NB = H // KP
NS = NB * PACK
QUADS = 4
STAGES = 3


def tile_list_hide_grading_board_kernel(tc, tab_words, tab_scales, offs, w1, w4_words, w4_scales, light, page0,
                                                 wgs, offs2, sc, offs3, gain, w2, offs4, base, out):
    nc = tc.nc
    cols = [slice(h * HALF, (h + 1) * HALF) for h in range(2)]
    entries = [slice(h * HALF // 16, (h + 1) * HALF // 16) for h in range(2)]

    def rows(ap, s):
        b, t = divmod(s, PACK)
        return ap.rearrange("(b p t) c -> b t p c", b=NB, t=PACK)[b, t]

    with ExitStack() as ctx:
        keep = ctx.enter_context(tc.tile_pool(name="keep", bufs=1))
        ring = ctx.enter_context(tc.tile_pool(name="ring", bufs=2))
        psum = ctx.enter_context(tc.psum_pool(name="psum", bufs=2))

        l_tab = keep.tile([P, S // 16], U16, name="l_tab")
        l_put = keep.tile([P, S // 16], U16, name="l_put")
        l_dye = keep.tile([P, NP // 16], U16, name="l_dye")
        l_herd = keep.tile([P, NP // 16], U16, name="l_herd")

        w4s_raw = keep.tile([P, H], U8, name="w4s_raw", align_bytes=64)
        tabs = keep.tile([P, T], U8, name="tabs", align_bytes=64)
        nc.gpsimd.memset(w4s_raw[:].bitcast(I32), 0)
        nc.vector.memset(tabs[:].bitcast(I32), 0)
        nc.sync.dma_start(l_tab[:], offs)
        w4_raw = keep.tile([P, 2 * H], U8, name="w4_raw", align_bytes=64)
        nc.sync.dma_start(out=w4_raw[:].bitcast(I32), in_=w4_words[0].bitcast(I32))
        sc_sb = keep.tile([P, NB, PACK], F32, name="sc_sb")
        gain_sb = keep.tile([P, NB, PACK], F32, name="gain_sb")

        def load_w(w, a, b):
            raw = ring.tile([P, PACK, KP], F32, name="w_raw", bufs=3)
            nc.sync.dma_start(out=raw[:], in_=w[a * KP : (a + 1) * KP, b * KP : (b + 1) * KP].rearrange("(p j) c -> p j c", j=PACK))
            return raw

        w1_first = load_w(w1, 0, 0)
        tabw = keep.tile([P, T], I32, name="tabw", tag="big_a", align_bytes=64)
        nc.sync.dma_start(out=tabw[:], in_=tab_words[0].rearrange("p t i -> p (t i)").bitcast(I32))
        for q in range(QUADS):
            nc.scalar.dma_start(out=w4s_raw[32 * q : 32 * q + 4, :].bitcast(I32), in_=w4_scales[0, 4 * q : 4 * q + 4, :].bitcast(I32))
        for q in range(QUADS):
            nc.gpsimd.dma_start(out=tabs[32 * q : 32 * q + 4, :].bitcast(I32), in_=tab_scales[0, 4 * q : 4 * q + 4, :].bitcast(I32))

        wgs_sb = keep.tile([P, PACK, S], F32, name="wgs_sb", tag="big_b", align_bytes=64)
        wgs_rows = wgs.rearrange("(q t) c -> q t c", t=PACK)

        def load_wgs(t):
            for q in (0, 2, 1, 3):
                nc.sync.dma_start(out=wgs_sb[32 * q : 32 * q + 32, t, :], in_=wgs_rows[:, t, :])

        def load_light(s):
            nc.sync.dma_start(out=work[s][:], in_=rows(light, s))

        pages = [keep.tile([P, T2], F32, name="page%d" % s) for s in range(NS)]
        work = [keep.tile([P, S], F32, name="work%d" % s) for s in range(NS)]
        load_light(0)
        load_wgs(0)
        nc.sync.dma_start(l_put[:], offs2)
        nc.sync.dma_start(out=pages[0][:], in_=rows(page0, 0))
        nc.sync.dma_start(l_dye[:], offs3)

        w4d = keep.tile([P, 2 * H], U8, name="w4d", align_bytes=64)
        w4sd = keep.tile([P, H], U8, name="w4sd", align_bytes=64)
        nc.vector.tensor_copy(out=w4d[:].rearrange("p (b t m e) -> p b t m e", b=NB, t=PACK, e=2),
                              in_=w4_raw[:].rearrange("p (b m t e) -> p b t m e", b=NB, t=PACK, e=2))
        nc.vector.tensor_copy(out=w4sd[:].rearrange("p (b t m) -> p b t m", b=NB, t=PACK),
                              in_=w4s_raw[:].rearrange("p (b m t) -> p b t m", b=NB, t=PACK))

        ident = keep.tile([P, P], F32, name="ident")
        make_identity(nc, ident[:])

        vw = [keep.tile([P, HALF], I32, name="vw%d" % h, align_bytes=64) for h in range(2)]
        vs = [keep.tile([P, HALF], U8, name="vs%d" % h, align_bytes=64) for h in range(2)]
        for h in range(2):
            nc.vector.tensor_copy(vw[h][:].bitcast(U32), tabw[:].bitcast(U32).indirect(l_tab[:, entries[h]]))
            nc.vector.tensor_copy(vs[h][:], tabs[:].indirect(l_tab[:, entries[h]]))

        w1c = [keep.tile([P, KP], I32, name="w1c%d" % b, align_bytes=64) for b in range(NB)]
        shared = keep.tile([P, 9 * P], U8, name="shared", align_bytes=64)

        def plane(row, col):
            return shared[row:P, col * P : col * P + KP]

        w1s = [plane(0, 1), plane(4, 3)]

        w2c = [[keep.tile([P, KP], I32, name="w2c%d%d" % (a, b), align_bytes=64) for b in range(NB)] for a in range(NB)]
        w2s = [[plane(8, 4), plane(8, 0)], [plane(12, 1), plane(12, 5)]]

        stage = [keep.tile([P, S], F32, name="stage%d" % i, align_bytes=64) for i in range(STAGES)]

        def cast_w(raw, grouped):
            nc.scalar.copy(out=grouped.rearrange("p (t m j) -> p m j t", t=PACK, j=PACK), in_=raw[:].rearrange("p j (m t) -> p m j t", t=PACK))

        larger = keep.tile([P, S], F32, name="larger")
        scaled = keep.tile([P, S], F32, name="scaled")
        grain_ps = {}

        def products(s):
            b, t = divmod(s, PACK)
            for h in range(2):
                flaw = psum.tile([P, HALF], F32, name="bank_a")
                nc.tensor.matmul_mx(out=flaw[:], lhsT=w4d[:, 2 * P * s : 2 * P * (s + 1)].bitcast(FP4X4), lhsT_scale=w4sd[:, P * s : P * (s + 1)],
                                    rhs=vw[h][:].bitcast(FP8X4), rhs_scale=vs[h][:], start=True, stop=True)
                grain = psum.tile([P, HALF], F32, name="bank_b")
                nc.tensor.matmul_mx(out=grain[:], lhsT=w1c[b][:, t * P : (t + 1) * P].bitcast(FP8X4), lhsT_scale=w1s[b][:, t * P : (t + 1) * P],
                                    rhs=vw[h][:].bitcast(FP8X4), rhs_scale=vs[h][:], start=True, stop=True)
                nc.scalar.copy(out=stage[s % STAGES][:, cols[h]], in_=flaw[:])
                grain_ps[s, h] = grain

        def scale_light(s, engine):
            engine.tensor_tensor(scaled[:], work[s][:], wgs_sb[:, s % PACK, :], ALU.mult)

        def take_larger(s):
            for h in range(2):
                nc.vector.tensor_tensor(larger[:, cols[h]], grain_ps[s, h][:], stage[s % STAGES][:, cols[h]], ALU.max)

        def put(s):
            nc.vector.tensor_tensor(pages[s][:].indirect(l_put[:]), larger[:], scaled[:], ALU.mult)

        quarters = {}

        def squash(s, h, picked):
            b, t = divmod(s, PACK)
            if (b, h) not in quarters:
                quarters[b, h] = ring.tile([P, PACK, HALF], BF16, name="quarter", bufs=NB * 2, align_bytes=64)
            sig = ring.tile([P, HALF], F32, name="sig")
            nc.scalar.activation(sig[:], picked, ACT.Sigmoid, scale=sc_sb[:, b, t : t + 1])
            nc.scalar.activation(quarters[b, h][:, t, :], sig[:], ACT.Copy, scale=gain_sb[:, b, t : t + 1])

        def pick(s, h, picked):
            nc.vector.tensor_copy(picked, pages[s][:].indirect(l_dye[:, entries[h]]))

        xc = [[keep.tile([P, HALF], I32, name="xc%d%d" % (b, h), align_bytes=64) for h in range(2)] for b in range(NB)]
        xs_own = [keep.tile([P, HALF], U8, name="xs%d" % i, align_bytes=64) for i in range(NB * 2 - 1)]
        xs = [[plane(0, 5), xs_own[0][:]], [xs_own[1][:], xs_own[2][:]]]

        def weave_x(b, h, woven, copy, c0, c1):
            copy(out=woven[:, PACK * c0 : PACK * c1].rearrange("p (c i t) -> p c t i", i=4, t=PACK),
                 in_=quarters[b, h][:, :, c0:c1].rearrange("p t (c i) -> p c t i", i=4))

        def quantise(codes, scales, values):
            nc.vector.quantize_mx(out=codes[:].bitcast(FP8X4), scales=scales, in_=values)

        weights = {0: (w1, 0, 1, w1c[1], w1s[1])}
        for i in range(NB * NB):
            a, b = divmod(i, NB)
            weights[1 + i] = (w2, a, b, w2c[a][b], w2s[a][b])
        raws = {}

        def load_slice(s):
            load_light(s)
            if s < PACK:
                load_wgs(s)
            if s in weights:
                raws[s] = load_w(*weights[s][:3])
            nc.sync.dma_start(out=pages[s][:], in_=rows(page0, s))

        raws[0] = load_w(*weights[0][:3])
        load_slice(1)
        nc.sync.dma_start(out=sc_sb[:], in_=sc.rearrange("(b p t) -> p b t", b=NB, t=PACK))
        nc.sync.dma_start(out=gain_sb[:], in_=gain.rearrange("(b p t) -> p b t", b=NB, t=PACK))
        nc.sync.dma_start(l_herd[:], offs4)

        first_in = stage[STAGES - 1][:].bitcast(BF16)
        cast_w(w1_first, first_in)
        quantise(w1c[0], w1s[0], first_in)
        products(0)
        scale_light(0, nc.vector)
        take_larger(0)
        products(1)
        for s in range(NS):
            if s + 2 < NS:
                load_slice(s + 2)
            spare = stage[s % STAGES][:].bitcast(BF16)
            if s in raws:
                cast_w(raws[s], spare)
                made = weights[s][3:]
            elif s + 1 < NS:
                h = s - len(weights)
                weave_x(0, h, spare, nc.scalar.copy, 0, HALF)
                made = (xc[0][h], xs[0][h])
            if s >= 1:
                for h in range(2 if s - 1 < PACK else 1):
                    squash(s - 1, h, work[s - 1][:, cols[h]])
            put(s)
            if s + 1 < NS:
                take_larger(s + 1)
                scale_light(s + 1, nc.gpsimd)
            if s + 2 < NS:
                products(s + 2)
            if s < PACK:
                nc.vector.tensor_copy(work[s][:], pages[s][:].indirect(l_dye[:]))
            else:
                pick(s, 0, work[s][:, cols[0]])
            if s + 1 < NS:
                quantise(made[0], made[1], spare)

        base_sb = [keep.tile([P, NB, PACK, HALF], F32, name="base%d" % h, tag=("big_a", "big_b")[h], align_bytes=64) for h in range(2)]
        for h in range(2):
            for b in range(NB):
                nc.sync.dma_start(out=base_sb[h][:, b], in_=base.rearrange("(b p t) c -> b p t c", b=NB, t=PACK)[b][:, :, cols[h]])

        last_stage = stage[(NS - 1) % STAGES]
        squash(NS - 1, 0, work[NS - 1][:, cols[0]])
        late = [larger[:, cols[0]], larger[:, cols[1]], last_stage[:, cols[0]], last_stage[:, cols[1]]]
        for t in range(PACK // 2):
            pick(PACK + t, 1, late[t])
        weave_x(1, 0, last_stage[:].bitcast(BF16), nc.scalar.copy, 0, HALF // 2)
        weave_x(1, 0, last_stage[:].bitcast(BF16), nc.vector.tensor_copy, HALF // 2, HALF)
        quantise(xc[1][0], xs[1][0], last_stage[:].bitcast(BF16))
        for t in range(PACK // 2, PACK):
            pick(PACK + t, 1, late[t])

        steps = [(h, s) for h in range(2) for s in range(NS)]

        def buffer_of(i, first, tiles):
            return work[first + i // 2 % tiles][:, cols[i % 2]]

        def multiply(i):
            h, s = steps[i]
            b, t = divmod(s, PACK)
            y = psum.tile([P, HALF], F32, name="y", bufs=4)
            for a in range(NB):
                nc.tensor.matmul_mx(out=y[:], lhsT=w2c[a][b][:, t * P : (t + 1) * P].bitcast(FP8X4), lhsT_scale=w2s[a][b][:, t * P : (t + 1) * P],
                                    rhs=xc[a][h][:].bitcast(FP8X4), rhs_scale=xs[a][h], start=(a == 0), stop=(a == NB - 1))
            ysc = buffer_of(i, 0, 2)
            nc.scalar.activation(ysc, y[:], ACT.Copy, scale=sc_sb[:, b, t : t + 1])
            nc.vector.tensor_tensor(product(i), pages[s][:].indirect(l_herd[:, entries[h]]), ysc, ALU.mult)

        def product(i):
            return buffer_of(i, 2, 2)

        def turned_sum(i):
            return buffer_of(i // 2, 4, 1)

        def base_of(i):
            h, s = steps[i]
            return base_sb[h][:, s // PACK, s % PACK, :]

        def store(i):
            h, s = steps[i]
            nc.sync.dma_start(out=rows(out, s)[:, cols[h]], in_=base_of(i))

        squares = [slice(c * P, (c + 1) * P) for c in range(HALF // P)]

        def add_turned(i):
            turned = psum.tile([P, HALF], F32, name="bank_a")
            for sq in squares:
                nc.tensor.matmul(turned[:, sq], base_of(i)[:, sq], ident[:], start=True, stop=False, is_transpose=True)
                nc.tensor.matmul(turned[:, sq], product(i)[:, sq], ident[:], start=False, stop=True, is_transpose=True)
            nc.scalar.copy(out=turned_sum(i), in_=turned[:])

        def turn_back(i):
            back = psum.tile([P, HALF], F32, name="bank_b")
            for sq in squares:
                nc.tensor.transpose(back[:, sq], turned_sum(i)[:, sq], ident[:])
            nc.scalar.copy(out=base_of(i), in_=back[:])
            store(i)

        n = len(steps)
        on_tensor = range(PACK + 1, n - 2, 2)
        for i in range(n + 1):
            if i < n:
                multiply(i)
            if i >= 1 and i - 1 not in on_tensor:
                nc.vector.tensor_tensor(base_of(i - 1), product(i - 1), base_of(i - 1), ALU.add)
                store(i - 1)
            if i - 2 in on_tensor:
                add_turned(i - 2)
            if i - 3 in on_tensor:
                turn_back(i - 3)
            if i < PACK:
                squash(PACK + i, 1, late[i])
            if i == PACK:
                last_in = stage[NS % STAGES][:].bitcast(BF16)
                weave_x(1, 1, last_in, nc.scalar.copy, 0, HALF)
                quantise(xc[1][1], xs[1][1], last_in)
